import numpy as np
import ml_dtypes


def mxq(x, axis, fmt="e4m3"):
    dtype, down = {"e4m3": (ml_dtypes.float8_e4m3fn, 7), "e5m2": (ml_dtypes.float8_e5m2, 14)}[fmt]
    v = np.moveaxis(np.asarray(x, np.float32).astype(ml_dtypes.bfloat16).astype(np.float64), axis, -1)
    blocks = v.reshape(v.shape[:-1] + (-1, 32))
    amax = np.abs(blocks).max(-1, keepdims=True)
    byte = np.maximum(np.where(amax > 0, np.frexp(amax)[1] - 1 + 127, 0) - down, 1)
    scale = np.exp2(byte - 127.0)
    codes = (blocks / scale).astype(np.float32).astype(dtype).astype(np.float64)
    return np.moveaxis((codes * scale).reshape(v.shape), -1, axis)


WIDE = False


def mx_kscale(k):
    if not WIDE:
        return np.ones(k)
    levels = np.array([10, -10, 5, -5, 0])
    if k % 512:
        return np.exp2(np.random.permutation(np.resize(levels, k // 32))).repeat(32)
    a = np.empty((k // 512, 16))
    for p in range(k // 512):
        a[p, :8] = np.random.permutation(np.resize(levels, 8))
        for g in range(8):
            far = levels[np.abs(levels - a[p, g]) >= 10]
            a[p, g + 8] = far[np.random.randint(len(far))]
    return np.exp2(a.ravel()).repeat(32)


def f64(x):
    return np.asarray(x).astype(np.float64)


def striped(idx):
    return np.tile(idx.reshape(-1, 16).T, (8, 1)).astype(np.uint16)


def unstriped(offs):
    return offs[:16].T.reshape(-1).astype(np.int64)


E2M1 = np.array([0.0, 0.5, 1.0, 1.5, 2.0, 3.0, 4.0, 6.0, -0.0, -0.5, -1.0, -1.5, -2.0, -3.0, -4.0, -6.0])


def pack_weight(w, fmt):
    k, n = w.shape
    w = f64(np.asarray(w, np.float32).astype(ml_dtypes.bfloat16)).reshape(k // 32, 32, n)
    amax = np.abs(w).max(1)
    if fmt == "e4m3":
        byte = np.frexp(amax)[1] - 1 + 127 - 7
    else:
        mant, ex = np.frexp(amax / 6.0)
        byte = np.where(mant > 0.5, ex, ex - 1) + 127
    byte = np.clip(np.where(amax > 0, byte, 1), 1, 254)
    scaled = (w * np.exp2(127.0 - byte)[:, None, :]).reshape(k, n).astype(np.float32)
    by_word = np.ascontiguousarray(scaled.reshape(k // 512, 128, 4, n).transpose(0, 1, 3, 2))
    if fmt == "e4m3":
        words = by_word.astype(ml_dtypes.float8_e4m3fn).view(np.uint8)
    else:
        c = by_word.astype(ml_dtypes.float4_e2m1fn).view(np.uint8) & 0xF
        words = (c[..., 0::2] | (c[..., 1::2] << 4)).reshape(k // 512, 128, 2 * n)
    return np.ascontiguousarray(words), np.ascontiguousarray(byte.astype(np.uint8).reshape(k // 512, 16, n))


def unpack_weight(words, scales, fmt):
    g, _, n = scales.shape
    words = np.ascontiguousarray(words).reshape(g, 128, n, -1)
    if fmt == "e4m3":
        vals = words.view(ml_dtypes.float8_e4m3fn).astype(np.float64)
    else:
        nib = np.empty((g, 128, n, 4), np.uint8)
        nib[..., 0::2] = words & 0xF
        nib[..., 1::2] = words >> 4
        vals = E2M1[nib]
    vals = vals * np.repeat(np.exp2(scales.astype(np.float64) - 127.0), 8, axis=1)[..., None]
    return vals.transpose(0, 1, 3, 2).reshape(g * 512, n)


def silu(v):
    return v / (1.0 + np.exp(-np.maximum(v, -700.0)))


def d_silu(v):
    s = 1.0 / (1.0 + np.exp(-np.maximum(v, -700.0)))
    return s * (1.0 + v * (1.0 - s))


K, T, E1, C1, E2, C2, H = 512, 768, 6, 128, 3, 256, 512
N = 1024


def by_expert(wq, xq, E, C):
    return np.concatenate([wq[e].T @ xq[:, e * C:(e + 1) * C] for e in range(E)], axis=1)


def setup_inputs():
    n = np.random.standard_normal
    v = mx_kscale(N)
    u = mx_kscale(H)
    slots1, slots2 = np.random.permutation(T), np.random.permutation(T)
    dy = pack_weight(n((N, T)) * v[:, None], "e4m3")
    w2t = pack_weight(n((N, H)) / np.sqrt(N) / v[:, None] * u, "e2m1")
    wat = [pack_weight(m, "e2m1") for m in n((E1, H, K)) / np.sqrt(H) / u[None, :, None]]
    wbt = [pack_weight(m, "e2m1") for m in n((E2, H, K)) / np.sqrt(H) / u[None, :, None]]
    return {
        "dy_words": dy[0],
        "dy_scales": dy[1],
        "w2t_words": w2t[0],
        "w2t_scales": w2t[1],
        "wat_words": np.stack([m[0] for m in wat]),
        "wat_scales": np.stack([m[1] for m in wat]),
        "wbt_words": np.stack([m[0] for m in wbt]),
        "wbt_scales": np.stack([m[1] for m in wbt]),
        "a": (n((H, T))).astype(np.float32),
        "c": (n((H, T))).astype(np.float32),
        "offs": striped(slots1),
        "offs2": striped(slots2),
    }


def reference(dy_words, dy_scales, w2t_words, w2t_scales, wat_words, wat_scales, wbt_words, wbt_scales, a, c, offs, offs2):
    w2t = unpack_weight(w2t_words, w2t_scales, "e2m1")
    wat = np.stack([unpack_weight(wat_words[e], wat_scales[e], "e2m1") for e in range(E1)])
    wbt = np.stack([unpack_weight(wbt_words[e], wbt_scales[e], "e2m1") for e in range(E2)])
    idx, idx2 = unstriped(offs), unstriped(offs2)
    dh = w2t.T @ unpack_weight(dy_words, dy_scales, "e4m3")
    da = dh * f64(c) * d_silu(f64(a))
    dc = dh * silu(f64(a))
    out = np.zeros((K, T))
    out[:, idx] = by_expert(wat, mxq(da[:, idx], 0, "e4m3"), E1, C1)
    out[:, idx2] += by_expert(wbt, mxq(dc[:, idx2], 0, "e4m3"), E2, C2)
    return out

@@ -1,0 +1,250 @@
+from contextlib import ExitStack
+
+import concourse.mybir as mybir
+
+K, T, H, N = 512, 768, 512, 1024
+E1, C1, E2, C2 = 6, 128, 3, 256
+FLOPS = 2 * N * H * T + 2 * 2 * H * K * T
+
+F32 = mybir.dt.float32
+BF16 = mybir.dt.bfloat16
+I32 = mybir.dt.int32
+U32 = mybir.dt.uint32
+U16 = mybir.dt.uint16
+U8 = mybir.dt.uint8
+FP8X4 = mybir.dt.float8_e4m3fn_x4
+FP4X4 = mybir.dt.float4_e2m1fn_x4
+ALU = mybir.AluOpType
+ACT = mybir.ActivationFunctionType
+
+P = 128
+PACK = 4
+PASSES = N // (P * PACK)
+PAIRS = 2
+CHUNK = 256
+CHUNKS = T // CHUNK
+KT = K // P
+BANK = 512
+HEAD = 256
+REST = T - HEAD
+PER_COL = 16
+
+
+def tile_moe_plb_silu_kernel(
+    tc, dy_words, dy_scales, w2t_words, w2t_scales, wat_words, wat_scales, wbt_words, wbt_scales, a, c, offs, offs2, out
+):
+    nc = tc.nc
+    with ExitStack() as ctx:
+        keep = ctx.enter_context(tc.tile_pool(name="keep", bufs=1))
+        psum = ctx.enter_context(tc.psum_pool(name="psum", bufs=1))
+
+        def sb(shape, dtype, name, tag=None):
+            return keep.tile(shape, dtype, name=name, tag=tag or name, align_bytes=64)
+
+        def bank(b, name):
+            return psum.tile([P, BANK], F32, name=name, tag="bank%d" % b)
+
+        def zeroed_plane(mats, width, name):
+            plane = sb([P, mats, width], U8, name)
+            nc.vector.memset(plane[:].bitcast(I32), 0)
+            return plane
+
+        def load_plane(plane, rows):
+            for r in range(4):
+                nc.sync.dma_start(out=plane[r:P:32, :, :].bitcast(I32), in_=rows[r].bitcast(I32))
+
+        w2s_raw = zeroed_plane(PASSES, H, "w2s_raw")
+        dys = zeroed_plane(PASSES, T, "dys")
+        wbs = zeroed_plane(E2, K, "wbs")
+        was = zeroed_plane(E1, K, "was")
+
+        w2_raw = sb([P, PASSES, 2 * H], U8, "w2_raw")
+        nc.sync.dma_start(out=w2_raw[:].bitcast(I32), in_=w2t_words.rearrange("s p n -> p s n").bitcast(I32))
+        load_plane(w2s_raw, w2t_scales.rearrange("s (q r) n -> r q s n", r=4))
+        dy_view = dy_words.rearrange("s p t d -> p s (t d)")
+        a_view = a.rearrange("(p j) t -> p j t", j=PACK)
+        c_view = c.rearrange("(p j) t -> p j t", j=PACK)
+        dy_sb, a_sb = {}, {}
+
+        def load_dy(n):
+            dy_sb[n] = sb([P, PASSES, CHUNK], U32, "dy%d" % n)
+            nc.sync.dma_start(
+                out=dy_sb[n][:].bitcast(I32), in_=dy_view[:, :, 4 * CHUNK * n : 4 * CHUNK * (n + 1)].bitcast(I32)
+            )
+
+        def load_a(q, n):
+            a_sb[q, n] = sb([P, 2, CHUNK], F32, "a%d%d" % (q, n))
+            nc.sync.dma_start(out=a_sb[q, n][:], in_=a_view[:, 2 * q : 2 * q + 2, CHUNK * n : CHUNK * (n + 1)])
+
+        load_dy(0)
+        load_plane(dys, dy_scales.rearrange("s (q r) t -> r q s t", r=4))
+        load_a(0, 0)
+        for n in range(1, CHUNKS):
+            load_dy(n)
+            load_a(0, n)
+        list2 = keep.tile([P, T // PER_COL], U16, name="list2")
+        nc.sync.dma_start(list2[:], offs2)
+        for n in range(CHUNKS):
+            load_a(1, n)
+        load_plane(wbs, wbt_scales.rearrange("e o (q r) k -> r q (e o) k", r=4))
+        wb = sb([P, E2, 2 * K], U8, "wb")
+        nc.sync.dma_start(out=wb[:].bitcast(I32), in_=wbt_words.rearrange("e o p n -> p (e o) n").bitcast(I32))
+        c_sb = []
+        for q in range(PAIRS):
+            c_sb.append(sb([P, 2, T], F32, "c%d" % q))
+            nc.sync.dma_start(out=c_sb[q][:], in_=c_view[:, 2 * q : 2 * q + 2, :])
+        list1 = keep.tile([P, T // PER_COL], U16, name="list1")
+        nc.sync.dma_start(list1[:], offs)
+        load_plane(was, wat_scales.rearrange("e o (q r) k -> r q (e o) k", r=4))
+        wa = sb([P, E1, 2 * K], U8, "wa")
+        nc.sync.dma_start(out=wa[:].bitcast(I32), in_=wat_words.rearrange("e o p n -> p (e o) n").bitcast(I32))
+
+        def entries(lst, lo, hi):
+            return lst[:, lo // PER_COL : hi // PER_COL]
+
+        w2, w2s = [], []
+        for q in range(PAIRS):
+            w2.append(sb([P, PASSES, 2, 2 * P], U8, "w2_%d" % q))
+            w2s.append(sb([P, PASSES, 2, P], U8, "w2s_%d" % q))
+            nc.vector.tensor_copy(
+                out=w2[q][:].bitcast(U16).rearrange("p s t (g i) -> p s g t i", i=8),
+                in_=w2_raw[:].bitcast(U16).rearrange("p s (g i t) -> p s g t i", i=8, t=PACK)[:, :, :, 2 * q : 2 * q + 2, :],
+            )
+            nc.vector.tensor_copy(
+                out=w2s[q][:].rearrange("p s t (g i) -> p s g t i", i=16),
+                in_=w2s_raw[:].rearrange("p s (g i t) -> p s g t i", i=16, t=PACK)[:, :, :, 2 * q : 2 * q + 2, :],
+            )
+
+        dh = {}
+        dc = [sb([P, T], U32, "dc%d" % q) for q in range(PAIRS)]
+        gb_head = sb([P, HEAD, 2], U32, "gb_head")
+        gb_planes = sb([P, 2, REST], U32, "gb_planes")
+        for q in range(PAIRS):
+            for n in range(CHUNKS):
+                dh[q, n] = bank(CHUNKS * q + n, "dh%d%d" % (q, n))
+                for t in range(2):
+                    for h in range(CHUNK // P):
+                        for s in range(PASSES):
+                            nc.tensor.matmul_mx(
+                                out=dh[q, n][:, CHUNK * t + P * h : CHUNK * t + P * (h + 1)],
+                                lhsT=w2[q][:, s, t, :].bitcast(FP4X4),
+                                lhsT_scale=w2s[q][:, s, t, :],
+                                rhs=dy_sb[n][:, s, P * h : P * (h + 1)].bitcast(FP8X4),
+                                rhs_scale=dys[:, s, CHUNK * n + P * h : CHUNK * n + P * (h + 1)],
+                                start=(s == 0),
+                                stop=(s == PASSES - 1),
+                            )
+                u = sb([P, CHUNK, 2], F32, "u%d%d" % (q, n))
+                nc.scalar.activation(out=u[:], in_=a_sb[q, n][:].rearrange("p j n -> p n j"), func=ACT.Silu)
+                nc.vector.tensor_tensor(
+                    out=dc[q][:, CHUNK * n : CHUNK * (n + 1)].bitcast(BF16).rearrange("p (n j) -> p n j", j=2),
+                    in0=dh[q, n][:].rearrange("p (j n) -> p n j", j=2),
+                    in1=u[:],
+                    op=ALU.mult,
+                )
+            nc.vector.tensor_copy(out=gb_head[:, :, q], in_=dc[q][:].indirect(entries(list2, 0, HEAD)))
+
+        def quantise(src, slots, name, tag=None):
+            codes = sb([P, slots], U32, name + "_codes", tag)
+            scales = sb([P, slots], U8, name + "_scales")
+            nc.vector.quantize_mx(out=codes[:].bitcast(FP8X4), scales=scales[:], in_=src)
+            return codes, scales
+
+        def expert_products(dst, words, planes, k, operand, first, count, width):
+            codes, scales = operand
+            for e in range(count):
+                nc.tensor.matmul_mx(
+                    out=dst[:, width * e : width * (e + 1)],
+                    lhsT=words[:, first + e, 2 * P * k : 2 * P * (k + 1)].bitcast(FP4X4),
+                    lhsT_scale=planes[:, first + e, P * k : P * (k + 1)],
+                    rhs=codes[:, width * e : width * (e + 1)].bitcast(FP8X4),
+                    rhs_scale=scales[:, width * e : width * (e + 1)],
+                    start=True,
+                    stop=True,
+                )
+
+        def head_results(banks, words, planes, operand, width, name):
+            staged = []
+            for half in range(2):
+                acc = bank(banks[half], "%s_acc%d" % (name, half))
+                for kk in range(2):
+                    expert_products(acc[:, HEAD * kk : HEAD * (kk + 1)], words, planes, 2 * half + kk, operand, 0, HEAD // width, width)
+                stage = sb([P, BANK], F32, "%s_stage%d" % (name, half))
+                nc.scalar.copy(out=stage[:], in_=acc[:])
+                staged += [stage[:, :HEAD], stage[:, HEAD:]]
+            return staged
+
+        def rest_results(b, words, planes, k, operand, width, name):
+            acc = bank(b, "%s_acc%d" % (name, k))
+            expert_products(acc, words, planes, k, operand, HEAD // width, REST // width, width)
+            stage = sb([P, REST], F32, "%s_stage%d" % (name, k))
+            nc.scalar.copy(out=stage[:], in_=acc[:])
+            return stage[:]
+
+        def scatter(window, lst, lo, hi, values):
+            nc.vector.tensor_copy(out=window[:].indirect(entries(lst, lo, hi)), in_=values)
+
+        qb_head = quantise(gb_head[:].rearrange("p n q -> p (n q)").bitcast(BF16), HEAD, "qb_head")
+        q_head = head_results((6, 7), wb, wbs, qb_head, C2, "q_head")
+        for q in range(PAIRS):
+            nc.vector.tensor_copy(out=gb_planes[:, q, :], in_=dc[q][:].indirect(entries(list2, HEAD, T)))
+        gb_rest = sb([P, REST, 2], U32, "gb_rest")
+        nc.scalar.copy(out=gb_rest[:], in_=gb_planes[:].rearrange("p q n -> p n q"))
+
+        q_win = [sb([P, T], F32, "q_win%d" % k) for k in range(KT)]
+        r_win = [sb([P, T], F32, "r_win%d" % k) for k in range(KT)]
+        scatter(q_win[0], list2, 0, HEAD, q_head[0])
+        qb_rest = quantise(gb_rest[:].rearrange("p n q -> p (n q)").bitcast(BF16), REST, "qb_rest")
+        for k in range(1, KT):
+            scatter(q_win[k], list2, 0, HEAD, q_head[k])
+        for k in range(2):
+            scatter(q_win[k], list2, HEAD, T, rest_results(6 + k, wb, wbs, k, qb_rest, C2, "q_rest"))
+
+        order = [(q, n) for q in range(PAIRS) for n in range(CHUNKS)]
+        v, sg = {}, {}
+        for q, n in order:
+            v[q, n] = sb([P, 2, CHUNK], F32, "v%d%d" % (q, n))
+            nc.scalar.activation(out=v[q, n][:], in_=a_sb[q, n][:], func=ACT.Silu, scale=-1.0)
+        for q, n in order:
+            sg[q, n] = sb([P, 2, CHUNK], F32, "sg%d%d" % (q, n))
+            nc.scalar.activation(out=sg[q, n][:], in_=a_sb[q, n][:], func=ACT.Sigmoid)
+        for q, n in order:
+            nc.vector.scalar_tensor_tensor(
+                out=v[q, n][:], in0=v[q, n][:], scalar=1.0, in1=c_sb[q][:, :, CHUNK * n : CHUNK * (n + 1)],
+                op0=ALU.subtract, op1=ALU.mult,
+            )
+        for q, n in order:
+            nc.vector.scalar_tensor_tensor(
+                out=sg[q, n][:], in0=v[q, n][:], scalar=-1.0, in1=sg[q, n][:], op0=ALU.mult, op1=ALU.mult,
+            )
+        da = sb([P, PACK, T], BF16, "da")
+        for q, n in order:
+            nc.vector.tensor_tensor(
+                out=da[:, 2 * q : 2 * q + 2, CHUNK * n : CHUNK * (n + 1)],
+                in0=dh[q, n][:].rearrange("p (j n) -> p j n", j=2),
+                in1=sg[q, n][:],
+                op=ALU.mult,
+            )
+
+        def gather_da(lo, hi, name):
+            g = sb([P, hi - lo, PACK], BF16, name)
+            for j in range(PACK):
+                nc.scalar.activation(out=g[:, :, j], in_=da[:, j, :].indirect(entries(list1, lo, hi)), func=ACT.Copy)
+            return g[:].rearrange("p n j -> p (n j)")
+
+        q_late = [rest_results(k, wb, wbs, k, qb_rest, C2, "q_rest") for k in range(2, KT)]
+        ga_head = gather_da(0, HEAD, "ga_head")
+        scatter(q_win[2], list2, HEAD, T, q_late[0])
+        qa_head = quantise(ga_head, HEAD, "qa_head", "q_rest_stage2")
+        r_head = head_results((0, 1), wa, was, qa_head, C1, "r_head")
+        ga_rest = gather_da(HEAD, T, "ga_rest")
+        scatter(q_win[3], list2, HEAD, T, q_late[1])
+        for k in range(2):
+            scatter(r_win[k], list1, 0, HEAD, r_head[k])
+        qa_rest = quantise(ga_rest, REST, "qa_rest", "r_head_stage0")
+        for k in range(2, KT):
+            scatter(r_win[k], list1, 0, HEAD, r_head[k])
+        for k in range(KT):
+            scatter(r_win[k], list1, HEAD, T, rest_results(4 + k, wa, was, k, qa_rest, C1, "r_rest"))
+            nc.vector.tensor_tensor(out=q_win[k][:], in0=q_win[k][:], in1=r_win[k][:], op=ALU.add)
+            nc.sync.dma_start(out=out[P * k : P * (k + 1), :], in_=q_win[k][:])

@@ -205,18 +205,16 @@ def tile_moe_plb_silu_kernel(
         for q, n in order:
             v[q, n] = sb([P, 2, CHUNK], F32, "v%d%d" % (q, n))
             nc.scalar.activation(out=v[q, n][:], in_=a_sb[q, n][:], func=ACT.Silu, scale=-1.0)
+            nc.scalar.activation(out=v[q, n][:], in_=v[q, n][:], func=ACT.Identity, scale=-1.0, bias=1.0)
         for q, n in order:
             sg[q, n] = sb([P, 2, CHUNK], F32, "sg%d%d" % (q, n))
             nc.scalar.activation(out=sg[q, n][:], in_=a_sb[q, n][:], func=ACT.Sigmoid)
         for q, n in order:
-            nc.vector.scalar_tensor_tensor(
-                out=v[q, n][:], in0=v[q, n][:], scalar=1.0, in1=c_sb[q][:, :, CHUNK * n : CHUNK * (n + 1)],
-                op0=ALU.subtract, op1=ALU.mult,
+            nc.gpsimd.tensor_tensor(
+                out=v[q, n][:], in0=v[q, n][:], in1=c_sb[q][:, :, CHUNK * n : CHUNK * (n + 1)], op=ALU.mult
             )
         for q, n in order:
-            nc.vector.scalar_tensor_tensor(
-                out=sg[q, n][:], in0=v[q, n][:], scalar=-1.0, in1=sg[q, n][:], op0=ALU.mult, op1=ALU.mult,
-            )
+            nc.gpsimd.tensor_tensor(out=sg[q, n][:], in0=v[q, n][:], in1=sg[q, n][:], op=ALU.mult)
         da = sb([P, PACK, T], BF16, "da")
         for q, n in order:
             nc.vector.tensor_tensor(
@@ -246,5 +244,6 @@ def tile_moe_plb_silu_kernel(
             scatter(r_win[k], list1, 0, HEAD, r_head[k])
         for k in range(KT):
             scatter(r_win[k], list1, HEAD, T, rest_results(4 + k, wa, was, k, qa_rest, C1, "r_rest"))
-            nc.vector.tensor_tensor(out=q_win[k][:], in0=q_win[k][:], in1=r_win[k][:], op=ALU.add)
+            adder = nc.vector if k == KT - 1 else nc.gpsimd
+            adder.tensor_tensor(out=q_win[k][:], in0=q_win[k][:], in1=r_win[k][:], op=ALU.add)
             nc.sync.dma_start(out=out[P * k : P * (k + 1), :], in_=q_win[k][:])

@@ -45,18 +45,16 @@ def tile_moe_plb_silu_kernel(
             return psum.tile([P, BANK], F32, name=name, tag="bank%d" % b)
 
         def zeroed_plane(mats, width, name):
-            plane = sb([P, mats, width], U8, name)
-            nc.vector.memset(plane[:].bitcast(I32), 0)
-            return plane
+            return sb([P, mats, width], U8, name)
 
-        def load_plane(plane, rows):
+        def load_plane(plane, rows, queues=None):
             for r in range(4):
-                nc.sync.dma_start(out=plane[r:P:32, :, :].bitcast(I32), in_=rows[r].bitcast(I32))
+                (queues[r] if queues else nc.sync).dma_start(out=plane[r:P:32, :, :].bitcast(I32), in_=rows[r].bitcast(I32))
 
         w2s_raw = zeroed_plane(PASSES, H, "w2s_raw")
+        nc.vector.memset(w2s_raw[:].bitcast(I32), 0)
         dys = zeroed_plane(PASSES, T, "dys")
-        wbs = zeroed_plane(E2, K, "wbs")
-        was = zeroed_plane(E1, K, "was")
+        nc.vector.memset(dys[:].bitcast(I32), 0)
 
         w2_raw = sb([P, PASSES, 2 * H], U8, "w2_raw")
         nc.sync.dma_start(out=w2_raw[:].bitcast(I32), in_=w2t_words.rearrange("s p n -> p s n").bitcast(I32))
@@ -64,7 +62,13 @@ def tile_moe_plb_silu_kernel(
         dy_view = dy_words.rearrange("s p t d -> p s (t d)")
         a_view = a.rearrange("(p j) t -> p j t", j=PACK)
         c_view = c.rearrange("(p j) t -> p j t", j=PACK)
-        dy_sb, a_sb = {}, {}
+        a_sb = {}
+
+        def load_a(q, n):
+            a_sb[q, n] = sb([P, 2, CHUNK], F32, "a%d%d" % (q, n))
+            nc.sync.dma_start(out=a_sb[q, n][:], in_=a_view[:, 2 * q : 2 * q + 2, CHUNK * n : CHUNK * (n + 1)])
+
+        dy_sb = {}
 
         def load_dy(n):
             dy_sb[n] = sb([P, PASSES, CHUNK], U32, "dy%d" % n)
@@ -72,27 +76,23 @@ def tile_moe_plb_silu_kernel(
                 out=dy_sb[n][:].bitcast(I32), in_=dy_view[:, :, 4 * CHUNK * n : 4 * CHUNK * (n + 1)].bitcast(I32)
             )
 
-        def load_a(q, n):
-            a_sb[q, n] = sb([P, 2, CHUNK], F32, "a%d%d" % (q, n))
-            nc.sync.dma_start(out=a_sb[q, n][:], in_=a_view[:, 2 * q : 2 * q + 2, CHUNK * n : CHUNK * (n + 1)])
-
         load_dy(0)
         load_plane(dys, dy_scales.rearrange("s (q r) t -> r q s t", r=4))
-        load_a(0, 0)
-        for n in range(1, CHUNKS):
-            load_dy(n)
-            load_a(0, n)
+        wbs = zeroed_plane(E2, K, "wbs")
+        was = zeroed_plane(E1, K, "was")
+        for n in range(CHUNKS):
+            if n:
+                load_dy(n)
+            for q in range(PAIRS):
+                load_a(q, n)
         list2 = keep.tile([P, T // PER_COL], U16, name="list2")
         nc.sync.dma_start(list2[:], offs2)
-        for n in range(CHUNKS):
-            load_a(1, n)
+        c_sb = [sb([P, 2, T], F32, "c%d" % q) for q in range(PAIRS)]
+        nc.sync.dma_start(out=c_sb[0][:], in_=c_view[:, 0:2, :])
         load_plane(wbs, wbt_scales.rearrange("e o (q r) k -> r q (e o) k", r=4))
         wb = sb([P, E2, 2 * K], U8, "wb")
         nc.sync.dma_start(out=wb[:].bitcast(I32), in_=wbt_words.rearrange("e o p n -> p (e o) n").bitcast(I32))
-        c_sb = []
-        for q in range(PAIRS):
-            c_sb.append(sb([P, 2, T], F32, "c%d" % q))
-            nc.sync.dma_start(out=c_sb[q][:], in_=c_view[:, 2 * q : 2 * q + 2, :])
+        nc.sync.dma_start(out=c_sb[1][:], in_=c_view[:, 2:4, :])
         list1 = keep.tile([P, T // PER_COL], U16, name="list1")
         nc.sync.dma_start(list1[:], offs)
         load_plane(was, wat_scales.rearrange("e o (q r) k -> r q (e o) k", r=4))
@@ -118,9 +118,8 @@ def tile_moe_plb_silu_kernel(
         dh = {}
         dc = [sb([P, T], U32, "dc%d" % q) for q in range(PAIRS)]
         gb_head = sb([P, HEAD, 2], U32, "gb_head")
-        gb_planes = sb([P, 2, REST], U32, "gb_planes")
-        for q in range(PAIRS):
-            for n in range(CHUNKS):
+        for n in range(CHUNKS):
+            for q in range(PAIRS):
                 dh[q, n] = bank(CHUNKS * q + n, "dh%d%d" % (q, n))
                 for t in range(2):
                     for h in range(CHUNK // P):
@@ -142,6 +141,7 @@ def tile_moe_plb_silu_kernel(
                     in1=u[:],
                     op=ALU.mult,
                 )
+        for q in range(PAIRS):
             nc.vector.tensor_copy(out=gb_head[:, :, q], in_=dc[q][:].indirect(entries(list2, 0, HEAD)))
 
         def quantise(src, slots, name, tag=None):
@@ -163,87 +163,117 @@ def tile_moe_plb_silu_kernel(
                     stop=True,
                 )
 
-        def head_results(banks, words, planes, operand, width, name):
-            staged = []
-            for half in range(2):
-                acc = bank(banks[half], "%s_acc%d" % (name, half))
-                for kk in range(2):
-                    expert_products(acc[:, HEAD * kk : HEAD * (kk + 1)], words, planes, 2 * half + kk, operand, 0, HEAD // width, width)
-                stage = sb([P, BANK], F32, "%s_stage%d" % (name, half))
-                nc.scalar.copy(out=stage[:], in_=acc[:])
-                staged += [stage[:, :HEAD], stage[:, HEAD:]]
-            return staged
-
-        def rest_results(b, words, planes, k, operand, width, name):
-            acc = bank(b, "%s_acc%d" % (name, k))
-            expert_products(acc, words, planes, k, operand, HEAD // width, REST // width, width)
-            stage = sb([P, REST], F32, "%s_stage%d" % (name, k))
-            nc.scalar.copy(out=stage[:], in_=acc[:])
-            return stage[:]
+        def results(b, words, planes, jobs, width, name, tag=None):
+            acc = bank(b, name + "_acc")
+            spans, at = [], 0
+            for k, operand, first, count in jobs:
+                expert_products(acc[:, at : at + width * count], words, planes, k, operand, first, count, width)
+                spans.append((at, at + width * count))
+                at += width * count
+            stage = sb([P, at], F32, name + "_stage", tag)
+            nc.scalar.copy(out=stage[:], in_=acc[:, :at])
+            return [stage[:, lo:hi] for lo, hi in spans]
 
         def scatter(window, lst, lo, hi, values):
             nc.vector.tensor_copy(out=window[:].indirect(entries(lst, lo, hi)), in_=values)
 
         qb_head = quantise(gb_head[:].rearrange("p n q -> p (n q)").bitcast(BF16), HEAD, "qb_head")
-        q_head = head_results((6, 7), wb, wbs, qb_head, C2, "q_head")
+        q_head = results(6, wb, wbs, [(0, qb_head, 0, 1), (1, qb_head, 0, 1)], C2, "q_head01")
+        acc = bank(7, "q_head23_acc")
+        for kk in range(2):
+            expert_products(acc[:, C2 * kk : C2 * (kk + 1)], wb, wbs, 2 + kk, qb_head, 0, 1, C2)
+        q2_all = sb([P, T], F32, "q2_all")
+        q3_head = sb([P, HEAD], F32, "q3_head")
+        nc.scalar.copy(out=q2_all[:, :HEAD], in_=acc[:, :C2])
+        nc.scalar.copy(out=q3_head[:], in_=acc[:, C2:])
+        gb_planes = sb([P, 2, REST], U32, "gb_planes", "gb_head")
         for q in range(PAIRS):
             nc.vector.tensor_copy(out=gb_planes[:, q, :], in_=dc[q][:].indirect(entries(list2, HEAD, T)))
-        gb_rest = sb([P, REST, 2], U32, "gb_rest")
-        nc.scalar.copy(out=gb_rest[:], in_=gb_planes[:].rearrange("p q n -> p n q"))
-
-        q_win = [sb([P, T], F32, "q_win%d" % k) for k in range(KT)]
-        r_win = [sb([P, T], F32, "r_win%d" % k) for k in range(KT)]
+        q_win = [sb([P, T], F32, "q_win0")]
         scatter(q_win[0], list2, 0, HEAD, q_head[0])
-        qb_rest = quantise(gb_rest[:].rearrange("p n q -> p (n q)").bitcast(BF16), REST, "qb_rest")
-        for k in range(1, KT):
-            scatter(q_win[k], list2, 0, HEAD, q_head[k])
-        for k in range(2):
-            scatter(q_win[k], list2, HEAD, T, rest_results(6 + k, wb, wbs, k, qb_rest, C2, "q_rest"))
 
         order = [(q, n) for q in range(PAIRS) for n in range(CHUNKS)]
-        v, sg = {}, {}
+        w_all = sb([P, PAIRS * CHUNKS, 2, CHUNK], F32, "w_all", "u02")
+        v = {qn: w_all[:, i, :, :] for i, qn in enumerate(order)}
         for q, n in order:
-            v[q, n] = sb([P, 2, CHUNK], F32, "v%d%d" % (q, n))
-            nc.scalar.activation(out=v[q, n][:], in_=a_sb[q, n][:], func=ACT.Silu, scale=-1.0)
-            nc.scalar.activation(out=v[q, n][:], in_=v[q, n][:], func=ACT.Identity, scale=-1.0, bias=1.0)
-        for q, n in order:
-            sg[q, n] = sb([P, 2, CHUNK], F32, "sg%d%d" % (q, n))
-            nc.scalar.activation(out=sg[q, n][:], in_=a_sb[q, n][:], func=ACT.Sigmoid)
-        for q, n in order:
-            nc.gpsimd.tensor_tensor(
-                out=v[q, n][:], in0=v[q, n][:], in1=c_sb[q][:, :, CHUNK * n : CHUNK * (n + 1)], op=ALU.mult
-            )
-        for q, n in order:
-            nc.gpsimd.tensor_tensor(out=sg[q, n][:], in0=v[q, n][:], in1=sg[q, n][:], op=ALU.mult)
-        da = sb([P, PACK, T], BF16, "da")
-        for q, n in order:
-            nc.vector.tensor_tensor(
-                out=da[:, 2 * q : 2 * q + 2, CHUNK * n : CHUNK * (n + 1)],
-                in0=dh[q, n][:].rearrange("p (j n) -> p j n", j=2),
-                in1=sg[q, n][:],
-                op=ALU.mult,
-            )
+            nc.scalar.activation(out=v[q, n], in_=a_sb[q, n][:], func=ACT.Silu, scale=-1.0)
+        gb_rest = sb([P, REST, 2], U32, "gb_rest")
+        nc.scalar.copy(out=gb_rest[:], in_=gb_planes[:].rearrange("p q n -> p n q"))
+        qb_rest = quantise(gb_rest[:].rearrange("p n q -> p (n q)").bitcast(BF16), REST, "qb_rest")
+        q_win.append(sb([P, T], F32, "q_win1", "gb_rest"))
+        dh_sb = [sb([P, BANK], F32, "dh_sb%d" % n, ("u12", "a00", "a01")[n]) for n in range(CHUNKS)]
+        nc.scalar.copy(out=dh_sb[0][:], in_=dh[1, 0][:])
+        scatter(q_win[1], list2, 0, HEAD, q_head[1])
+        for n in range(CHUNKS):
+            nc.scalar.activation(out=v[1, n], in_=v[1, n], func=ACT.Identity, scale=-1.0, bias=1.0)
+        q_rest = [results(6 + k, wb, wbs, [(k, qb_rest, 1, 2)], C2, "q_rest%d" % k)[0] for k in range(2)]
+        for k in range(2):
+            scatter(q_win[k], list2, HEAD, T, q_rest[k])
+        sg_pair = [sb([P, CHUNKS, 2, CHUNK], F32, "sg%d" % q, ("gb_head", "a02")[q]) for q in range(PAIRS)]
+        sg = {(q, n): sg_pair[q][:, n, :, :] for q, n in order}
+        for n in range(CHUNKS):
+            nc.scalar.activation(out=sg[0, n], in_=a_sb[0, n][:], func=ACT.Sigmoid)
+        acc = bank(6, "q_rest2_acc")
+        expert_products(acc, wb, wbs, 2, qb_rest, 1, 2, C2)
+        nc.scalar.copy(out=q2_all[:, HEAD:], in_=acc[:])
+        for n in range(CHUNKS):
+            nc.scalar.activation(out=sg[1, n], in_=a_sb[1, n][:], func=ACT.Sigmoid)
+        for n in range(1, CHUNKS):
+            nc.scalar.copy(out=dh_sb[n][:], in_=dh[1, n][:])
 
-        def gather_da(lo, hi, name):
-            g = sb([P, hi - lo, PACK], BF16, name)
-            for j in range(PACK):
-                nc.scalar.activation(out=g[:, :, j], in_=da[:, j, :].indirect(entries(list1, lo, hi)), func=ACT.Copy)
-            return g[:].rearrange("p n j -> p (n j)")
+        for q, n in order:
+            if q == 0:
+                nc.gpsimd.tensor_scalar(out=v[q, n], in0=v[q, n], scalar1=-1.0, scalar2=1.0, op0=ALU.mult, op1=ALU.add)
+            nc.gpsimd.tensor_tensor(out=v[q, n], in0=v[q, n], in1=c_sb[q][:, :, CHUNK * n : CHUNK * (n + 1)], op=ALU.mult)
+        for q, n in order:
+            nc.gpsimd.tensor_tensor(out=sg[q, n], in0=v[q, n], in1=sg[q, n], op=ALU.mult)
+        da = [sb([P, 2, T], BF16, "da%d" % q, ("q_rest1_stage", "da1")[q]) for q in range(PAIRS)]
+        ga_head = sb([P, HEAD, PACK], BF16, "ga_head")
+        ga_rest = sb([P, REST, PACK], BF16, "ga_rest")
 
-        q_late = [rest_results(k, wb, wbs, k, qb_rest, C2, "q_rest") for k in range(2, KT)]
-        ga_head = gather_da(0, HEAD, "ga_head")
-        scatter(q_win[2], list2, HEAD, T, q_late[0])
-        qa_head = quantise(ga_head, HEAD, "qa_head", "q_rest_stage2")
-        r_head = head_results((0, 1), wa, was, qa_head, C1, "r_head")
-        ga_rest = gather_da(HEAD, T, "ga_rest")
-        scatter(q_win[3], list2, HEAD, T, q_late[1])
+        def da_pair(engine, q, sums):
+            for n in range(CHUNKS):
+                engine.tensor_tensor(
+                    out=da[q][:, :, CHUNK * n : CHUNK * (n + 1)],
+                    in0=sums[n][:].rearrange("p (j n) -> p j n", j=2),
+                    in1=sg[q, n],
+                    op=ALU.mult,
+                )
+
+        def gather_da(dst, q, lo, hi):
+            for j in range(2):
+                nc.scalar.activation(out=dst[:, :, 2 * q + j], in_=da[q][:, j, :].indirect(entries(list1, lo, hi)), func=ACT.Copy)
+
+        da_pair(nc.vector, 0, [dh[0, n] for n in range(CHUNKS)])
+        gather_da(ga_head, 0, 0, HEAD)
+        gather_da(ga_rest, 0, HEAD, T)
+        q_win.append(sb([P, 1024], F32, "q_win2", "gb_head"))
+        scatter(q_win[2], list2, 0, T, q2_all[:])
+        da_pair(nc.gpsimd, 1, dh_sb)
+        gather_da(ga_head, 1, 0, HEAD)
+        q_last = results(7, wb, wbs, [(3, qb_rest, 1, 2)], C2, "q_rest3", "a02")[0]
+        q_win.append(sb([P, T], F32, "q_win3", "q2_all"))
+        scatter(q_win[3], list2, 0, HEAD, q3_head[:])
+        qa_head = quantise(ga_head[:].rearrange("p n j -> p (n j)"), HEAD, "qa_head", "q3_head")
+        r_head = results(0, wa, was, [(0, qa_head, 0, 2), (1, qa_head, 0, 2)], C1, "r_head01")
+        r_head += results(1, wa, was, [(2, qa_head, 0, 2), (3, qa_head, 0, 2)], C1, "r_head23")
+        gather_da(ga_rest, 1, HEAD, T)
+        scatter(q_win[3], list2, HEAD, T, q_last)
+        r_win = [sb([P, T], F32, "r_win%d" % k) for k in range(KT - 1)]
         for k in range(2):
             scatter(r_win[k], list1, 0, HEAD, r_head[k])
-        qa_rest = quantise(ga_rest, REST, "qa_rest", "r_head_stage0")
+        qa_rest = quantise(ga_rest[:].rearrange("p n j -> p (n j)"), REST, "qa_rest", "r_head01_stage")
+        r_win.append(sb([P, T], F32, "r_win3", "ga_rest"))
         for k in range(2, KT):
             scatter(r_win[k], list1, 0, HEAD, r_head[k])
         for k in range(KT):
-            scatter(r_win[k], list1, HEAD, T, rest_results(4 + k, wa, was, k, qa_rest, C1, "r_rest"))
-            adder = nc.vector if k == KT - 1 else nc.gpsimd
-            adder.tensor_tensor(out=q_win[k][:], in0=q_win[k][:], in1=r_win[k][:], op=ALU.add)
-            nc.sync.dma_start(out=out[P * k : P * (k + 1), :], in_=q_win[k][:])
+            scatter(r_win[k], list1, HEAD, T, results(4 + k, wa, was, [(k, qa_rest, 2, 4)], C1, "r_rest%d" % k)[0])
+            if k < KT - 1:
+                nc.gpsimd.tensor_tensor(out=r_win[k][:], in0=q_win[k][:, :T], in1=r_win[k][:], op=ALU.add)
+                nc.sync.dma_start(out=out[P * k : P * (k + 1), :], in_=r_win[k][:])
+            else:
+                for half, queue in enumerate((nc.sync, nc.scalar)):
+                    cols = slice(T // 2 * half, T // 2 * (half + 1))
+                    total = sb([P, T // 2], F32, "total%d" % half)
+                    nc.vector.tensor_tensor(out=total[:], in0=q_win[k][:, cols], in1=r_win[k][:, cols], op=ALU.add)
+                    queue.dma_start(out=out[P * k : P * (k + 1), cols], in_=total[:])

@@ -20,14 +20,17 @@ ACT = mybir.ActivationFunctionType
 P = 128
 PACK = 4
 PASSES = N // (P * PACK)
-PAIRS = 2
-CHUNK = 256
+PAIRS = PACK // 2
+BANK = 512
+CHUNK = BANK // 2
 CHUNKS = T // CHUNK
 KT = K // P
-BANK = 512
-HEAD = 256
+HEAD = C2
 REST = T - HEAD
 PER_COL = 16
+QUADRANT = 32
+WIDE = 1024
+LINE = 16
 
 
 def tile_moe_plb_silu_kernel(
@@ -44,236 +47,238 @@ def tile_moe_plb_silu_kernel(
         def bank(b, name):
             return psum.tile([P, BANK], F32, name=name, tag="bank%d" % b)
 
-        def zeroed_plane(mats, width, name):
-            return sb([P, mats, width], U8, name)
+        def load_scale_rows(planes, rows, which=range(4)):
+            for r in which:
+                nc.sync.dma_start(out=planes[r:P:QUADRANT, :, :].bitcast(I32), in_=rows[r].bitcast(I32))
 
-        def load_plane(plane, rows, queues=None):
-            for r in range(4):
-                (queues[r] if queues else nc.sync).dma_start(out=plane[r:P:32, :, :].bitcast(I32), in_=rows[r].bitcast(I32))
-
-        w2s_raw = zeroed_plane(PASSES, H, "w2s_raw")
+        w2s_raw = sb([P, PASSES, H], U8, "w2s_raw")
         nc.vector.memset(w2s_raw[:].bitcast(I32), 0)
-        dys = zeroed_plane(PASSES, T, "dys")
-        nc.vector.memset(dys[:].bitcast(I32), 0)
+        dys = sb([P, PASSES, T], U8, "dys")
 
         w2_raw = sb([P, PASSES, 2 * H], U8, "w2_raw")
         nc.sync.dma_start(out=w2_raw[:].bitcast(I32), in_=w2t_words.rearrange("s p n -> p s n").bitcast(I32))
-        load_plane(w2s_raw, w2t_scales.rearrange("s (q r) n -> r q s n", r=4))
-        dy_view = dy_words.rearrange("s p t d -> p s (t d)")
-        a_view = a.rearrange("(p j) t -> p j t", j=PACK)
-        c_view = c.rearrange("(p j) t -> p j t", j=PACK)
-        a_sb = {}
-
-        def load_a(q, n):
-            a_sb[q, n] = sb([P, 2, CHUNK], F32, "a%d%d" % (q, n))
-            nc.sync.dma_start(out=a_sb[q, n][:], in_=a_view[:, 2 * q : 2 * q + 2, CHUNK * n : CHUNK * (n + 1)])
-
-        dy_sb = {}
-
-        def load_dy(n):
-            dy_sb[n] = sb([P, PASSES, CHUNK], U32, "dy%d" % n)
-            nc.sync.dma_start(
-                out=dy_sb[n][:].bitcast(I32), in_=dy_view[:, :, 4 * CHUNK * n : 4 * CHUNK * (n + 1)].bitcast(I32)
-            )
-
-        load_dy(0)
-        load_plane(dys, dy_scales.rearrange("s (q r) t -> r q s t", r=4))
-        wbs = zeroed_plane(E2, K, "wbs")
-        was = zeroed_plane(E1, K, "was")
-        for n in range(CHUNKS):
-            if n:
-                load_dy(n)
-            for q in range(PAIRS):
-                load_a(q, n)
+        load_scale_rows(w2s_raw, w2t_scales.rearrange("s (q r) n -> r q s n", r=4))
+        dys_rows = dy_scales.rearrange("s (q r) t -> r q s t", r=4)
+        load_scale_rows(dys, dys_rows, (0, 1))
+        dy = sb([P, PASSES, T], U32, "dy")
+        nc.sync.dma_start(out=dy[:].bitcast(I32), in_=dy_words.rearrange("s p t d -> p s (t d)").bitcast(I32))
+        load_scale_rows(dys, dys_rows, (2, 3))
         list2 = keep.tile([P, T // PER_COL], U16, name="list2")
         nc.sync.dma_start(list2[:], offs2)
-        c_sb = [sb([P, 2, T], F32, "c%d" % q) for q in range(PAIRS)]
-        nc.sync.dma_start(out=c_sb[0][:], in_=c_view[:, 0:2, :])
-        load_plane(wbs, wbt_scales.rearrange("e o (q r) k -> r q (e o) k", r=4))
+        wbs = sb([P, E2, K], U8, "wbs")
+        was = sb([P, E1, K], U8, "was")
+        a_view = a.rearrange("(p j) t -> p j t", j=PACK)
+        c_view = c.rearrange("(p j) t -> p j t", j=PACK)
+        a_pair = [sb([P, 2, T], F32, "a%d" % q) for q in range(PAIRS)]
+        for q in range(PAIRS):
+            nc.sync.dma_start(out=a_pair[q][:], in_=a_view[:, 2 * q : 2 * q + 2, :])
+        load_scale_rows(wbs, wbt_scales.rearrange("e o (q r) k -> r q (e o) k", r=4))
         wb = sb([P, E2, 2 * K], U8, "wb")
         nc.sync.dma_start(out=wb[:].bitcast(I32), in_=wbt_words.rearrange("e o p n -> p (e o) n").bitcast(I32))
-        nc.sync.dma_start(out=c_sb[1][:], in_=c_view[:, 2:4, :])
+        c_pair = [sb([P, 2, T], F32, "c%d" % q) for q in range(PAIRS)]
+        for q in range(PAIRS):
+            nc.sync.dma_start(out=c_pair[q][:], in_=c_view[:, 2 * q : 2 * q + 2, :])
         list1 = keep.tile([P, T // PER_COL], U16, name="list1")
         nc.sync.dma_start(list1[:], offs)
-        load_plane(was, wat_scales.rearrange("e o (q r) k -> r q (e o) k", r=4))
+        load_scale_rows(was, wat_scales.rearrange("e o (q r) k -> r q (e o) k", r=4))
         wa = sb([P, E1, 2 * K], U8, "wa")
         nc.sync.dma_start(out=wa[:].bitcast(I32), in_=wat_words.rearrange("e o p n -> p (e o) n").bitcast(I32))
 
         def entries(lst, lo, hi):
             return lst[:, lo // PER_COL : hi // PER_COL]
 
+        def tokens(n):
+            return slice(CHUNK * n, CHUNK * (n + 1))
+
         w2, w2s = [], []
         for q in range(PAIRS):
+            pair = slice(2 * q, 2 * q + 2)
             w2.append(sb([P, PASSES, 2, 2 * P], U8, "w2_%d" % q))
             w2s.append(sb([P, PASSES, 2, P], U8, "w2s_%d" % q))
             nc.vector.tensor_copy(
-                out=w2[q][:].bitcast(U16).rearrange("p s t (g i) -> p s g t i", i=8),
-                in_=w2_raw[:].bitcast(U16).rearrange("p s (g i t) -> p s g t i", i=8, t=PACK)[:, :, :, 2 * q : 2 * q + 2, :],
+                out=w2[q][:].bitcast(U16).rearrange("p s j (g i) -> p s g j i", i=LINE // 2),
+                in_=w2_raw[:].bitcast(U16).rearrange("p s (g i j) -> p s g j i", i=LINE // 2, j=PACK)[:, :, :, pair, :],
             )
             nc.vector.tensor_copy(
-                out=w2s[q][:].rearrange("p s t (g i) -> p s g t i", i=16),
-                in_=w2s_raw[:].rearrange("p s (g i t) -> p s g t i", i=16, t=PACK)[:, :, :, 2 * q : 2 * q + 2, :],
+                out=w2s[q][:].rearrange("p s j (g i) -> p s g j i", i=LINE),
+                in_=w2s_raw[:].rearrange("p s (g i j) -> p s g j i", i=LINE, j=PACK)[:, :, :, pair, :],
             )
 
         dh = {}
         dc = [sb([P, T], U32, "dc%d" % q) for q in range(PAIRS)]
-        gb_head = sb([P, HEAD, 2], U32, "gb_head")
-        for n in range(CHUNKS):
-            for q in range(PAIRS):
+        dc_head = sb([P, HEAD, 2], U32, "dc_head")
+        for q in range(PAIRS):
+            for n in range(CHUNKS):
                 dh[q, n] = bank(CHUNKS * q + n, "dh%d%d" % (q, n))
-                for t in range(2):
-                    for h in range(CHUNK // P):
+                for j in range(2):
+                    for half in range(CHUNK // P):
+                        cols = slice(CHUNK * n + P * half, CHUNK * n + P * (half + 1))
                         for s in range(PASSES):
                             nc.tensor.matmul_mx(
-                                out=dh[q, n][:, CHUNK * t + P * h : CHUNK * t + P * (h + 1)],
-                                lhsT=w2[q][:, s, t, :].bitcast(FP4X4),
-                                lhsT_scale=w2s[q][:, s, t, :],
-                                rhs=dy_sb[n][:, s, P * h : P * (h + 1)].bitcast(FP8X4),
-                                rhs_scale=dys[:, s, CHUNK * n + P * h : CHUNK * n + P * (h + 1)],
+                                out=dh[q, n][:, CHUNK * j + P * half : CHUNK * j + P * (half + 1)],
+                                lhsT=w2[q][:, s, j, :].bitcast(FP4X4),
+                                lhsT_scale=w2s[q][:, s, j, :],
+                                rhs=dy[:, s, cols].bitcast(FP8X4),
+                                rhs_scale=dys[:, s, cols],
                                 start=(s == 0),
                                 stop=(s == PASSES - 1),
                             )
-                u = sb([P, CHUNK, 2], F32, "u%d%d" % (q, n))
-                nc.scalar.activation(out=u[:], in_=a_sb[q, n][:].rearrange("p j n -> p n j"), func=ACT.Silu)
+                silu_a = sb([P, CHUNK, 2], F32, "silu%d%d" % (q, n))
+                nc.scalar.activation(
+                    out=silu_a[:], in_=a_pair[q][:, :, tokens(n)].rearrange("p j n -> p n j"), func=ACT.Silu
+                )
                 nc.vector.tensor_tensor(
-                    out=dc[q][:, CHUNK * n : CHUNK * (n + 1)].bitcast(BF16).rearrange("p (n j) -> p n j", j=2),
+                    out=dc[q][:, tokens(n)].bitcast(BF16).rearrange("p (n j) -> p n j", j=2),
                     in0=dh[q, n][:].rearrange("p (j n) -> p n j", j=2),
-                    in1=u[:],
+                    in1=silu_a[:],
                     op=ALU.mult,
                 )
-        for q in range(PAIRS):
-            nc.vector.tensor_copy(out=gb_head[:, :, q], in_=dc[q][:].indirect(entries(list2, 0, HEAD)))
+            nc.vector.tensor_copy(out=dc_head[:, :, q], in_=dc[q][:].indirect(entries(list2, 0, HEAD)))
 
-        def quantise(src, slots, name, tag=None):
+        def quantise(values, slots, name, tag=None):
             codes = sb([P, slots], U32, name + "_codes", tag)
             scales = sb([P, slots], U8, name + "_scales")
-            nc.vector.quantize_mx(out=codes[:].bitcast(FP8X4), scales=scales[:], in_=src)
+            nc.vector.quantize_mx(out=codes[:].bitcast(FP8X4), scales=scales[:], in_=values)
             return codes, scales
 
         def expert_products(dst, words, planes, k, operand, first, count, width):
             codes, scales = operand
             for e in range(count):
+                cols = slice(width * e, width * (e + 1))
                 nc.tensor.matmul_mx(
-                    out=dst[:, width * e : width * (e + 1)],
+                    out=dst[:, cols],
                     lhsT=words[:, first + e, 2 * P * k : 2 * P * (k + 1)].bitcast(FP4X4),
                     lhsT_scale=planes[:, first + e, P * k : P * (k + 1)],
-                    rhs=codes[:, width * e : width * (e + 1)].bitcast(FP8X4),
-                    rhs_scale=scales[:, width * e : width * (e + 1)],
+                    rhs=codes[:, cols].bitcast(FP8X4),
+                    rhs_scale=scales[:, cols],
                     start=True,
                     stop=True,
                 )
 
-        def results(b, words, planes, jobs, width, name, tag=None):
+        def results(b, words, planes, row_tiles, operand, first, count, width, name):
             acc = bank(b, name + "_acc")
-            spans, at = [], 0
-            for k, operand, first, count in jobs:
-                expert_products(acc[:, at : at + width * count], words, planes, k, operand, first, count, width)
-                spans.append((at, at + width * count))
-                at += width * count
-            stage = sb([P, at], F32, name + "_stage", tag)
-            nc.scalar.copy(out=stage[:], in_=acc[:, :at])
-            return [stage[:, lo:hi] for lo, hi in spans]
+            span = width * count
+            for i, k in enumerate(row_tiles):
+                expert_products(acc[:, span * i : span * (i + 1)], words, planes, k, operand, first, count, width)
+            stage = sb([P, span * len(row_tiles)], F32, name + "_stage")
+            nc.scalar.copy(out=stage[:], in_=acc[:, : span * len(row_tiles)])
+            return [stage[:, span * i : span * (i + 1)] for i in range(len(row_tiles))]
 
         def scatter(window, lst, lo, hi, values):
             nc.vector.tensor_copy(out=window[:].indirect(entries(lst, lo, hi)), in_=values)
 
-        qb_head = quantise(gb_head[:].rearrange("p n q -> p (n q)").bitcast(BF16), HEAD, "qb_head")
-        q_head = results(6, wb, wbs, [(0, qb_head, 0, 1), (1, qb_head, 0, 1)], C2, "q_head01")
+        head_experts2, rest_experts2 = HEAD // C2, REST // C2
+        mx_dc_head = quantise(dc_head[:].rearrange("p n q -> p (n q)").bitcast(BF16), HEAD, "mx_dc_head")
+        q_head = results(6, wb, wbs, (0, 1), mx_dc_head, 0, head_experts2, C2, "q_head01")
         acc = bank(7, "q_head23_acc")
-        for kk in range(2):
-            expert_products(acc[:, C2 * kk : C2 * (kk + 1)], wb, wbs, 2 + kk, qb_head, 0, 1, C2)
+        for i, k in enumerate((2, 3)):
+            expert_products(acc[:, HEAD * i : HEAD * (i + 1)], wb, wbs, k, mx_dc_head, 0, head_experts2, C2)
         q2_all = sb([P, T], F32, "q2_all")
         q3_head = sb([P, HEAD], F32, "q3_head")
-        nc.scalar.copy(out=q2_all[:, :HEAD], in_=acc[:, :C2])
-        nc.scalar.copy(out=q3_head[:], in_=acc[:, C2:])
-        gb_planes = sb([P, 2, REST], U32, "gb_planes", "gb_head")
+        nc.scalar.copy(out=q2_all[:, :HEAD], in_=acc[:, :HEAD])
+        nc.scalar.copy(out=q3_head[:], in_=acc[:, HEAD:])
+        dc_rest_pairs = sb([P, 2, REST], U32, "dc_rest_pairs", "dc_head")
         for q in range(PAIRS):
-            nc.vector.tensor_copy(out=gb_planes[:, q, :], in_=dc[q][:].indirect(entries(list2, HEAD, T)))
+            nc.vector.tensor_copy(out=dc_rest_pairs[:, q, :], in_=dc[q][:].indirect(entries(list2, HEAD, T)))
         q_win = [sb([P, T], F32, "q_win0")]
         scatter(q_win[0], list2, 0, HEAD, q_head[0])
 
         order = [(q, n) for q in range(PAIRS) for n in range(CHUNKS)]
-        w_all = sb([P, PAIRS * CHUNKS, 2, CHUNK], F32, "w_all", "u02")
-        v = {qn: w_all[:, i, :, :] for i, qn in enumerate(order)}
+        gain_all = sb([P, PAIRS * CHUNKS, 2, CHUNK], F32, "gain_all", "silu11")
+        gain = {qn: gain_all[:, i, :, :] for i, qn in enumerate(order)}
         for q, n in order:
-            nc.scalar.activation(out=v[q, n], in_=a_sb[q, n][:], func=ACT.Silu, scale=-1.0)
-        gb_rest = sb([P, REST, 2], U32, "gb_rest")
-        nc.scalar.copy(out=gb_rest[:], in_=gb_planes[:].rearrange("p q n -> p n q"))
-        qb_rest = quantise(gb_rest[:].rearrange("p n q -> p (n q)").bitcast(BF16), REST, "qb_rest")
-        q_win.append(sb([P, T], F32, "q_win1", "gb_rest"))
-        dh_sb = [sb([P, BANK], F32, "dh_sb%d" % n, ("u12", "a00", "a01")[n]) for n in range(CHUNKS)]
-        nc.scalar.copy(out=dh_sb[0][:], in_=dh[1, 0][:])
+            nc.scalar.activation(out=gain[q, n], in_=a_pair[q][:, :, tokens(n)], func=ACT.Silu, scale=-1.0)
+
+        dc_rest = sb([P, REST, 2], U32, "dc_rest")
+        nc.scalar.copy(out=dc_rest[:], in_=dc_rest_pairs[:].rearrange("p q n -> p n q"))
+        mx_dc_rest = quantise(dc_rest[:].rearrange("p n q -> p (n q)").bitcast(BF16), REST, "mx_dc_rest")
+        q_win.append(sb([P, T], F32, "q_win1", "dc_rest"))
+        dh_sb = sb([P, BANK], F32, "dh_sb", "silu12")
+        nc.scalar.copy(out=dh_sb[:], in_=dh[1, 0][:])
         scatter(q_win[1], list2, 0, HEAD, q_head[1])
         for n in range(CHUNKS):
-            nc.scalar.activation(out=v[1, n], in_=v[1, n], func=ACT.Identity, scale=-1.0, bias=1.0)
-        q_rest = [results(6 + k, wb, wbs, [(k, qb_rest, 1, 2)], C2, "q_rest%d" % k)[0] for k in range(2)]
+            nc.scalar.activation(out=gain[1, n], in_=gain[1, n], func=ACT.Identity, scale=-1.0, bias=1.0)
+        q_rest = [
+            results(6 + k, wb, wbs, (k,), mx_dc_rest, head_experts2, rest_experts2, C2, "q_rest%d" % k)[0]
+            for k in range(2)
+        ]
         for k in range(2):
             scatter(q_win[k], list2, HEAD, T, q_rest[k])
-        sg_pair = [sb([P, CHUNKS, 2, CHUNK], F32, "sg%d" % q, ("gb_head", "a02")[q]) for q in range(PAIRS)]
-        sg = {(q, n): sg_pair[q][:, n, :, :] for q, n in order}
+
+        factor_pair = [sb([P, CHUNKS, 2, CHUNK], F32, "factor%d" % q, ("dc_head", "a0")[q]) for q in range(PAIRS)]
+        factor = {(q, n): factor_pair[q][:, n, :, :] for q, n in order}
         for n in range(CHUNKS):
-            nc.scalar.activation(out=sg[0, n], in_=a_sb[0, n][:], func=ACT.Sigmoid)
+            nc.scalar.activation(out=factor[0, n], in_=a_pair[0][:, :, tokens(n)], func=ACT.Sigmoid)
         acc = bank(6, "q_rest2_acc")
-        expert_products(acc, wb, wbs, 2, qb_rest, 1, 2, C2)
+        expert_products(acc, wb, wbs, 2, mx_dc_rest, head_experts2, rest_experts2, C2)
         nc.scalar.copy(out=q2_all[:, HEAD:], in_=acc[:])
         for n in range(CHUNKS):
-            nc.scalar.activation(out=sg[1, n], in_=a_sb[1, n][:], func=ACT.Sigmoid)
-        for n in range(1, CHUNKS):
-            nc.scalar.copy(out=dh_sb[n][:], in_=dh[1, n][:])
-
+            nc.scalar.activation(out=factor[1, n], in_=a_pair[1][:, :, tokens(n)], func=ACT.Sigmoid)
         for q, n in order:
             if q == 0:
-                nc.gpsimd.tensor_scalar(out=v[q, n], in0=v[q, n], scalar1=-1.0, scalar2=1.0, op0=ALU.mult, op1=ALU.add)
-            nc.gpsimd.tensor_tensor(out=v[q, n], in0=v[q, n], in1=c_sb[q][:, :, CHUNK * n : CHUNK * (n + 1)], op=ALU.mult)
-        for q, n in order:
-            nc.gpsimd.tensor_tensor(out=sg[q, n], in0=v[q, n], in1=sg[q, n], op=ALU.mult)
-        da = [sb([P, 2, T], BF16, "da%d" % q, ("q_rest1_stage", "da1")[q]) for q in range(PAIRS)]
-        ga_head = sb([P, HEAD, PACK], BF16, "ga_head")
-        ga_rest = sb([P, REST, PACK], BF16, "ga_rest")
-
-        def da_pair(engine, q, sums):
-            for n in range(CHUNKS):
-                engine.tensor_tensor(
-                    out=da[q][:, :, CHUNK * n : CHUNK * (n + 1)],
-                    in0=sums[n][:].rearrange("p (j n) -> p j n", j=2),
-                    in1=sg[q, n],
-                    op=ALU.mult,
+                nc.gpsimd.tensor_scalar(
+                    out=gain[q, n], in0=gain[q, n], scalar1=-1.0, scalar2=1.0, op0=ALU.mult, op1=ALU.add
                 )
+            nc.gpsimd.tensor_tensor(out=gain[q, n], in0=gain[q, n], in1=c_pair[q][:, :, tokens(n)], op=ALU.mult)
+        for q, n in order:
+            nc.gpsimd.tensor_tensor(out=factor[q, n], in0=gain[q, n], in1=factor[q, n], op=ALU.mult)
+
+        da = [sb([P, 2, T], BF16, "da%d" % q, ("q_rest1_stage", "da1")[q]) for q in range(PAIRS)]
+        da_head = sb([P, HEAD, PACK], BF16, "da_head")
+        da_rest = sb([P, REST, PACK], BF16, "da_rest")
+
+        def da_chunk(engine, q, n, sums):
+            engine.tensor_tensor(
+                out=da[q][:, :, tokens(n)],
+                in0=sums[:].rearrange("p (j n) -> p j n", j=2),
+                in1=factor[q, n],
+                op=ALU.mult,
+            )
 
         def gather_da(dst, q, lo, hi):
             for j in range(2):
-                nc.scalar.activation(out=dst[:, :, 2 * q + j], in_=da[q][:, j, :].indirect(entries(list1, lo, hi)), func=ACT.Copy)
+                nc.scalar.activation(
+                    out=dst[:, :, 2 * q + j], in_=da[q][:, j, :].indirect(entries(list1, lo, hi)), func=ACT.Copy
+                )
 
-        da_pair(nc.vector, 0, [dh[0, n] for n in range(CHUNKS)])
-        gather_da(ga_head, 0, 0, HEAD)
-        gather_da(ga_rest, 0, HEAD, T)
-        q_win.append(sb([P, 1024], F32, "q_win2", "gb_head"))
+        for n in range(CHUNKS):
+            da_chunk(nc.vector, 0, n, dh[0, n])
+        gather_da(da_head, 0, 0, HEAD)
+        gather_da(da_rest, 0, HEAD, T)
+        q_win.append(sb([P, WIDE], F32, "q_win2", "dc_head"))
         scatter(q_win[2], list2, 0, T, q2_all[:])
-        da_pair(nc.gpsimd, 1, dh_sb)
-        gather_da(ga_head, 1, 0, HEAD)
-        q_last = results(7, wb, wbs, [(3, qb_rest, 1, 2)], C2, "q_rest3", "a02")[0]
-        q_win.append(sb([P, T], F32, "q_win3", "q2_all"))
+        da_chunk(nc.gpsimd, 1, 0, dh_sb)
+        for n in range(1, CHUNKS):
+            da_chunk(nc.vector, 1, n, dh[1, n])
+        gather_da(da_head, 1, 0, HEAD)
+
+        q3_rest = results(5, wb, wbs, (3,), mx_dc_rest, head_experts2, rest_experts2, C2, "q_rest3")[0]
+        q_win.append(sb([P, T], F32, "q_win3", "a0"))
         scatter(q_win[3], list2, 0, HEAD, q3_head[:])
-        qa_head = quantise(ga_head[:].rearrange("p n j -> p (n j)"), HEAD, "qa_head", "q3_head")
-        r_head = results(0, wa, was, [(0, qa_head, 0, 2), (1, qa_head, 0, 2)], C1, "r_head01")
-        r_head += results(1, wa, was, [(2, qa_head, 0, 2), (3, qa_head, 0, 2)], C1, "r_head23")
-        gather_da(ga_rest, 1, HEAD, T)
-        scatter(q_win[3], list2, HEAD, T, q_last)
+        head_experts1, rest_experts1 = HEAD // C1, REST // C1
+        mx_da_head = quantise(da_head[:].rearrange("p n j -> p (n j)"), HEAD, "mx_da_head", "q3_head")
+        r_head = results(0, wa, was, (0, 1), mx_da_head, 0, head_experts1, C1, "r_head01")
+        r_head += results(1, wa, was, (2, 3), mx_da_head, 0, head_experts1, C1, "r_head23")
+        gather_da(da_rest, 1, HEAD, T)
+        scatter(q_win[3], list2, HEAD, T, q3_rest)
+
         r_win = [sb([P, T], F32, "r_win%d" % k) for k in range(KT - 1)]
         for k in range(2):
             scatter(r_win[k], list1, 0, HEAD, r_head[k])
-        qa_rest = quantise(ga_rest[:].rearrange("p n j -> p (n j)"), REST, "qa_rest", "r_head01_stage")
-        r_win.append(sb([P, T], F32, "r_win3", "ga_rest"))
+        mx_da_rest = quantise(da_rest[:].rearrange("p n j -> p (n j)"), REST, "mx_da_rest", "r_head01_stage")
+        r_win.append(sb([P, T], F32, "r_win3", "da_rest"))
         for k in range(2, KT):
             scatter(r_win[k], list1, 0, HEAD, r_head[k])
         for k in range(KT):
-            scatter(r_win[k], list1, HEAD, T, results(4 + k, wa, was, [(k, qa_rest, 2, 4)], C1, "r_rest%d" % k)[0])
+            r_rest = results(4 + k, wa, was, (k,), mx_da_rest, head_experts1, rest_experts1, C1, "r_rest%d" % k)[0]
+            scatter(r_win[k], list1, HEAD, T, r_rest)
+            rows = slice(P * k, P * (k + 1))
             if k < KT - 1:
                 nc.gpsimd.tensor_tensor(out=r_win[k][:], in0=q_win[k][:, :T], in1=r_win[k][:], op=ALU.add)
-                nc.sync.dma_start(out=out[P * k : P * (k + 1), :], in_=r_win[k][:])
+                nc.sync.dma_start(out=out[rows, :], in_=r_win[k][:])
             else:
                 for half, queue in enumerate((nc.sync, nc.scalar)):
                     cols = slice(T // 2 * half, T // 2 * (half + 1))
                     total = sb([P, T // 2], F32, "total%d" % half)
                     nc.vector.tensor_tensor(out=total[:], in0=q_win[k][:, cols], in1=r_win[k][:, cols], op=ALU.add)
-                    queue.dma_start(out=out[P * k : P * (k + 1), cols], in_=total[:])
+                    queue.dma_start(out=out[rows, cols], in_=total[:])

from contextlib import ExitStack

import concourse.mybir as mybir

K, T, H, N = 512, 768, 512, 1024
E1, C1, E2, C2 = 6, 128, 3, 256
FLOPS = 2 * N * H * T + 2 * 2 * H * K * T

F32 = mybir.dt.float32
BF16 = mybir.dt.bfloat16
I32 = mybir.dt.int32
U32 = mybir.dt.uint32
U16 = mybir.dt.uint16
U8 = mybir.dt.uint8
FP8X4 = mybir.dt.float8_e4m3fn_x4
FP4X4 = mybir.dt.float4_e2m1fn_x4
ALU = mybir.AluOpType
ACT = mybir.ActivationFunctionType

P = 128
PACK = 4
PASSES = N // (P * PACK)
PAIRS = PACK // 2
BANK = 512
CHUNK = BANK // 2
CHUNKS = T // CHUNK
KT = K // P
HEAD = C2
REST = T - HEAD
PER_COL = 16
QUADRANT = 32
WIDE = 1024
LINE = 16


def tile_moe_plb_silu_kernel(
    tc, dy_words, dy_scales, w2t_words, w2t_scales, wat_words, wat_scales, wbt_words, wbt_scales, a, c, offs, offs2, out
):
    nc = tc.nc
    with ExitStack() as ctx:
        keep = ctx.enter_context(tc.tile_pool(name="keep", bufs=1))
        psum = ctx.enter_context(tc.psum_pool(name="psum", bufs=1))

        def sb(shape, dtype, name, tag=None):
            return keep.tile(shape, dtype, name=name, tag=tag or name, align_bytes=64)

        def bank(b, name):
            return psum.tile([P, BANK], F32, name=name, tag="bank%d" % b)

        def load_scale_rows(planes, rows, which=range(4)):
            for r in which:
                nc.sync.dma_start(out=planes[r:P:QUADRANT, :, :].bitcast(I32), in_=rows[r].bitcast(I32))

        w2s_raw = sb([P, PASSES, H], U8, "w2s_raw")
        nc.vector.memset(w2s_raw[:].bitcast(I32), 0)
        dys = sb([P, PASSES, T], U8, "dys")

        w2_raw = sb([P, PASSES, 2 * H], U8, "w2_raw")
        nc.sync.dma_start(out=w2_raw[:].bitcast(I32), in_=w2t_words.rearrange("s p n -> p s n").bitcast(I32))
        load_scale_rows(w2s_raw, w2t_scales.rearrange("s (q r) n -> r q s n", r=4))
        dys_rows = dy_scales.rearrange("s (q r) t -> r q s t", r=4)
        load_scale_rows(dys, dys_rows, (0, 1))
        dy = sb([P, PASSES, T], U32, "dy")
        nc.sync.dma_start(out=dy[:].bitcast(I32), in_=dy_words.rearrange("s p t d -> p s (t d)").bitcast(I32))
        load_scale_rows(dys, dys_rows, (2, 3))
        list2 = keep.tile([P, T // PER_COL], U16, name="list2")
        nc.sync.dma_start(list2[:], offs2)
        wbs = sb([P, E2, K], U8, "wbs")
        was = sb([P, E1, K], U8, "was")
        a_view = a.rearrange("(p j) t -> p j t", j=PACK)
        c_view = c.rearrange("(p j) t -> p j t", j=PACK)
        a_pair = [sb([P, 2, T], F32, "a%d" % q) for q in range(PAIRS)]
        for q in range(PAIRS):
            nc.sync.dma_start(out=a_pair[q][:], in_=a_view[:, 2 * q : 2 * q + 2, :])
        load_scale_rows(wbs, wbt_scales.rearrange("e o (q r) k -> r q (e o) k", r=4))
        wb = sb([P, E2, 2 * K], U8, "wb")
        nc.sync.dma_start(out=wb[:].bitcast(I32), in_=wbt_words.rearrange("e o p n -> p (e o) n").bitcast(I32))
        c_pair = [sb([P, 2, T], F32, "c%d" % q) for q in range(PAIRS)]
        for q in range(PAIRS):
            nc.sync.dma_start(out=c_pair[q][:], in_=c_view[:, 2 * q : 2 * q + 2, :])
        list1 = keep.tile([P, T // PER_COL], U16, name="list1")
        nc.sync.dma_start(list1[:], offs)
        load_scale_rows(was, wat_scales.rearrange("e o (q r) k -> r q (e o) k", r=4))
        wa = sb([P, E1, 2 * K], U8, "wa")
        nc.sync.dma_start(out=wa[:].bitcast(I32), in_=wat_words.rearrange("e o p n -> p (e o) n").bitcast(I32))

        def entries(lst, lo, hi):
            return lst[:, lo // PER_COL : hi // PER_COL]

        def tokens(n):
            return slice(CHUNK * n, CHUNK * (n + 1))

        w2, w2s = [], []
        for q in range(PAIRS):
            pair = slice(2 * q, 2 * q + 2)
            w2.append(sb([P, PASSES, 2, 2 * P], U8, "w2_%d" % q))
            w2s.append(sb([P, PASSES, 2, P], U8, "w2s_%d" % q))
            nc.vector.tensor_copy(
                out=w2[q][:].bitcast(U16).rearrange("p s j (g i) -> p s g j i", i=LINE // 2),
                in_=w2_raw[:].bitcast(U16).rearrange("p s (g i j) -> p s g j i", i=LINE // 2, j=PACK)[:, :, :, pair, :],
            )
            nc.vector.tensor_copy(
                out=w2s[q][:].rearrange("p s j (g i) -> p s g j i", i=LINE),
                in_=w2s_raw[:].rearrange("p s (g i j) -> p s g j i", i=LINE, j=PACK)[:, :, :, pair, :],
            )

        dh = {}
        dc = [sb([P, T], U32, "dc%d" % q) for q in range(PAIRS)]
        dc_head = sb([P, HEAD, 2], U32, "dc_head")
        for q in range(PAIRS):
            for n in range(CHUNKS):
                dh[q, n] = bank(CHUNKS * q + n, "dh%d%d" % (q, n))
                for j in range(2):
                    for half in range(CHUNK // P):
                        cols = slice(CHUNK * n + P * half, CHUNK * n + P * (half + 1))
                        for s in range(PASSES):
                            nc.tensor.matmul_mx(
                                out=dh[q, n][:, CHUNK * j + P * half : CHUNK * j + P * (half + 1)],
                                lhsT=w2[q][:, s, j, :].bitcast(FP4X4),
                                lhsT_scale=w2s[q][:, s, j, :],
                                rhs=dy[:, s, cols].bitcast(FP8X4),
                                rhs_scale=dys[:, s, cols],
                                start=(s == 0),
                                stop=(s == PASSES - 1),
                            )
                silu_a = sb([P, CHUNK, 2], F32, "silu%d%d" % (q, n))
                nc.scalar.activation(
                    out=silu_a[:], in_=a_pair[q][:, :, tokens(n)].rearrange("p j n -> p n j"), func=ACT.Silu
                )
                nc.vector.tensor_tensor(
                    out=dc[q][:, tokens(n)].bitcast(BF16).rearrange("p (n j) -> p n j", j=2),
                    in0=dh[q, n][:].rearrange("p (j n) -> p n j", j=2),
                    in1=silu_a[:],
                    op=ALU.mult,
                )
            nc.vector.tensor_copy(out=dc_head[:, :, q], in_=dc[q][:].indirect(entries(list2, 0, HEAD)))

        def quantise(values, slots, name, tag=None):
            codes = sb([P, slots], U32, name + "_codes", tag)
            scales = sb([P, slots], U8, name + "_scales")
            nc.vector.quantize_mx(out=codes[:].bitcast(FP8X4), scales=scales[:], in_=values)
            return codes, scales

        def expert_products(dst, words, planes, k, operand, first, count, width):
            codes, scales = operand
            for e in range(count):
                cols = slice(width * e, width * (e + 1))
                nc.tensor.matmul_mx(
                    out=dst[:, cols],
                    lhsT=words[:, first + e, 2 * P * k : 2 * P * (k + 1)].bitcast(FP4X4),
                    lhsT_scale=planes[:, first + e, P * k : P * (k + 1)],
                    rhs=codes[:, cols].bitcast(FP8X4),
                    rhs_scale=scales[:, cols],
                    start=True,
                    stop=True,
                )

        def results(b, words, planes, row_tiles, operand, first, count, width, name):
            acc = bank(b, name + "_acc")
            span = width * count
            for i, k in enumerate(row_tiles):
                expert_products(acc[:, span * i : span * (i + 1)], words, planes, k, operand, first, count, width)
            stage = sb([P, span * len(row_tiles)], F32, name + "_stage")
            nc.scalar.copy(out=stage[:], in_=acc[:, : span * len(row_tiles)])
            return [stage[:, span * i : span * (i + 1)] for i in range(len(row_tiles))]

        def scatter(window, lst, lo, hi, values):
            nc.vector.tensor_copy(out=window[:].indirect(entries(lst, lo, hi)), in_=values)

        head_experts2, rest_experts2 = HEAD // C2, REST // C2
        mx_dc_head = quantise(dc_head[:].rearrange("p n q -> p (n q)").bitcast(BF16), HEAD, "mx_dc_head")
        q_head = results(6, wb, wbs, (0, 1), mx_dc_head, 0, head_experts2, C2, "q_head01")
        acc = bank(7, "q_head23_acc")
        for i, k in enumerate((2, 3)):
            expert_products(acc[:, HEAD * i : HEAD * (i + 1)], wb, wbs, k, mx_dc_head, 0, head_experts2, C2)
        q2_all = sb([P, T], F32, "q2_all")
        q3_head = sb([P, HEAD], F32, "q3_head")
        nc.scalar.copy(out=q2_all[:, :HEAD], in_=acc[:, :HEAD])
        nc.scalar.copy(out=q3_head[:], in_=acc[:, HEAD:])
        dc_rest_pairs = sb([P, 2, REST], U32, "dc_rest_pairs", "dc_head")
        for q in range(PAIRS):
            nc.vector.tensor_copy(out=dc_rest_pairs[:, q, :], in_=dc[q][:].indirect(entries(list2, HEAD, T)))
        q_win = [sb([P, T], F32, "q_win0")]
        scatter(q_win[0], list2, 0, HEAD, q_head[0])

        order = [(q, n) for q in range(PAIRS) for n in range(CHUNKS)]
        gain_all = sb([P, PAIRS * CHUNKS, 2, CHUNK], F32, "gain_all", "silu11")
        gain = {qn: gain_all[:, i, :, :] for i, qn in enumerate(order)}
        for q, n in order:
            nc.scalar.activation(out=gain[q, n], in_=a_pair[q][:, :, tokens(n)], func=ACT.Silu, scale=-1.0)

        dc_rest = sb([P, REST, 2], U32, "dc_rest")
        nc.scalar.copy(out=dc_rest[:], in_=dc_rest_pairs[:].rearrange("p q n -> p n q"))
        mx_dc_rest = quantise(dc_rest[:].rearrange("p n q -> p (n q)").bitcast(BF16), REST, "mx_dc_rest")
        q_win.append(sb([P, T], F32, "q_win1", "dc_rest"))
        dh_sb = sb([P, BANK], F32, "dh_sb", "silu12")
        nc.scalar.copy(out=dh_sb[:], in_=dh[1, 0][:])
        scatter(q_win[1], list2, 0, HEAD, q_head[1])
        for n in range(CHUNKS):
            nc.scalar.activation(out=gain[1, n], in_=gain[1, n], func=ACT.Identity, scale=-1.0, bias=1.0)
        q_rest = [
            results(6 + k, wb, wbs, (k,), mx_dc_rest, head_experts2, rest_experts2, C2, "q_rest%d" % k)[0]
            for k in range(2)
        ]
        for k in range(2):
            scatter(q_win[k], list2, HEAD, T, q_rest[k])

        factor_pair = [sb([P, CHUNKS, 2, CHUNK], F32, "factor%d" % q, ("dc_head", "a0")[q]) for q in range(PAIRS)]
        factor = {(q, n): factor_pair[q][:, n, :, :] for q, n in order}
        for n in range(CHUNKS):
            nc.scalar.activation(out=factor[0, n], in_=a_pair[0][:, :, tokens(n)], func=ACT.Sigmoid)
        acc = bank(6, "q_rest2_acc")
        expert_products(acc, wb, wbs, 2, mx_dc_rest, head_experts2, rest_experts2, C2)
        nc.scalar.copy(out=q2_all[:, HEAD:], in_=acc[:])
        for n in range(CHUNKS):
            nc.scalar.activation(out=factor[1, n], in_=a_pair[1][:, :, tokens(n)], func=ACT.Sigmoid)
        for q, n in order:
            if q == 0:
                nc.gpsimd.tensor_scalar(
                    out=gain[q, n], in0=gain[q, n], scalar1=-1.0, scalar2=1.0, op0=ALU.mult, op1=ALU.add
                )
            nc.gpsimd.tensor_tensor(out=gain[q, n], in0=gain[q, n], in1=c_pair[q][:, :, tokens(n)], op=ALU.mult)
        for q, n in order:
            nc.gpsimd.tensor_tensor(out=factor[q, n], in0=gain[q, n], in1=factor[q, n], op=ALU.mult)

        da = [sb([P, 2, T], BF16, "da%d" % q, ("q_rest1_stage", "da1")[q]) for q in range(PAIRS)]
        da_head = sb([P, HEAD, PACK], BF16, "da_head")
        da_rest = sb([P, REST, PACK], BF16, "da_rest")

        def da_chunk(engine, q, n, sums):
            engine.tensor_tensor(
                out=da[q][:, :, tokens(n)],
                in0=sums[:].rearrange("p (j n) -> p j n", j=2),
                in1=factor[q, n],
                op=ALU.mult,
            )

        def gather_da(dst, q, lo, hi):
            for j in range(2):
                nc.scalar.activation(
                    out=dst[:, :, 2 * q + j], in_=da[q][:, j, :].indirect(entries(list1, lo, hi)), func=ACT.Copy
                )

        for n in range(CHUNKS):
            da_chunk(nc.vector, 0, n, dh[0, n])
        gather_da(da_head, 0, 0, HEAD)
        gather_da(da_rest, 0, HEAD, T)
        q_win.append(sb([P, WIDE], F32, "q_win2", "dc_head"))
        scatter(q_win[2], list2, 0, T, q2_all[:])
        da_chunk(nc.gpsimd, 1, 0, dh_sb)
        for n in range(1, CHUNKS):
            da_chunk(nc.vector, 1, n, dh[1, n])
        gather_da(da_head, 1, 0, HEAD)

        q3_rest = results(5, wb, wbs, (3,), mx_dc_rest, head_experts2, rest_experts2, C2, "q_rest3")[0]
        q_win.append(sb([P, T], F32, "q_win3", "a0"))
        scatter(q_win[3], list2, 0, HEAD, q3_head[:])
        head_experts1, rest_experts1 = HEAD // C1, REST // C1
        mx_da_head = quantise(da_head[:].rearrange("p n j -> p (n j)"), HEAD, "mx_da_head", "q3_head")
        r_head = results(0, wa, was, (0, 1), mx_da_head, 0, head_experts1, C1, "r_head01")
        r_head += results(1, wa, was, (2, 3), mx_da_head, 0, head_experts1, C1, "r_head23")
        gather_da(da_rest, 1, HEAD, T)
        scatter(q_win[3], list2, HEAD, T, q3_rest)

        r_win = [sb([P, T], F32, "r_win%d" % k) for k in range(KT - 1)]
        for k in range(2):
            scatter(r_win[k], list1, 0, HEAD, r_head[k])
        mx_da_rest = quantise(da_rest[:].rearrange("p n j -> p (n j)"), REST, "mx_da_rest", "r_head01_stage")
        r_win.append(sb([P, T], F32, "r_win3", "da_rest"))
        for k in range(2, KT):
            scatter(r_win[k], list1, 0, HEAD, r_head[k])
        for k in range(KT):
            r_rest = results(4 + k, wa, was, (k,), mx_da_rest, head_experts1, rest_experts1, C1, "r_rest%d" % k)[0]
            scatter(r_win[k], list1, HEAD, T, r_rest)
            rows = slice(P * k, P * (k + 1))
            if k < KT - 1:
                nc.gpsimd.tensor_tensor(out=r_win[k][:], in0=q_win[k][:, :T], in1=r_win[k][:], op=ALU.add)
                nc.sync.dma_start(out=out[rows, :], in_=r_win[k][:])
            else:
                for half, queue in enumerate((nc.sync, nc.scalar)):
                    cols = slice(T // 2 * half, T // 2 * (half + 1))
                    total = sb([P, T // 2], F32, "total%d" % half)
                    nc.vector.tensor_tensor(out=total[:], in0=q_win[k][:, cols], in1=r_win[k][:, cols], op=ALU.add)
                    queue.dma_start(out=out[rows, cols], in_=total[:])
